import numpy as np
import ml_dtypes


def mxq(x, axis, fmt="e4m3"):
    dtype, down = {"e4m3": (ml_dtypes.float8_e4m3fn, 7), "e5m2": (ml_dtypes.float8_e5m2, 14)}[fmt]
    v = np.moveaxis(np.asarray(x, np.float32).astype(ml_dtypes.bfloat16).astype(np.float64), axis, -1)
    blocks = v.reshape(v.shape[:-1] + (-1, 32))
    amax = np.abs(blocks).max(-1, keepdims=True)
    byte = np.maximum(np.where(amax > 0, np.frexp(amax)[1] - 1 + 127, 0) - down, 1)
    scale = np.exp2(byte - 127.0)
    codes = (blocks / scale).astype(np.float32).astype(dtype).astype(np.float64)
    return np.moveaxis((codes * scale).reshape(v.shape), -1, axis)


WIDE = False


def mx_kscale(k):
    if not WIDE:
        return np.ones(k)
    levels = np.array([10, -10, 5, -5, 0])
    if k % 512:
        return np.exp2(np.random.permutation(np.resize(levels, k // 32))).repeat(32)
    a = np.empty((k // 512, 16))
    for p in range(k // 512):
        a[p, :8] = np.random.permutation(np.resize(levels, 8))
        for g in range(8):
            far = levels[np.abs(levels - a[p, g]) >= 10]
            a[p, g + 8] = far[np.random.randint(len(far))]
    return np.exp2(a.ravel()).repeat(32)


def f64(x):
    return np.asarray(x).astype(np.float64)


def striped(idx):
    return np.tile(np.asarray(idx).reshape(-1, 16).T, (8, 1)).astype(np.uint16)


def unstriped(offs):
    return offs[:16].T.reshape(-1).astype(np.int64)


def striped8(idx):
    return np.asarray(idx).reshape(8, -1, 16).transpose(0, 2, 1).reshape(128, -1).astype(np.uint16)


def unstriped8(offs):
    return offs.reshape(8, 16, -1).transpose(0, 2, 1).reshape(8, -1).astype(np.int64)


def pick8(x, idx, run):
    r = np.arange(len(x))
    return x[r[:, None], idx[r % (8 * run) // run]]


E2M1 = np.array([0.0, 0.5, 1.0, 1.5, 2.0, 3.0, 4.0, 6.0, -0.0, -0.5, -1.0, -1.5, -2.0, -3.0, -4.0, -6.0])


def pack_weight(w, fmt):
    k, n = w.shape
    w = f64(np.asarray(w, np.float32).astype(ml_dtypes.bfloat16)).reshape(k // 32, 32, n)
    amax = np.abs(w).max(1)
    if fmt == "e4m3":
        byte = np.frexp(amax)[1] - 1 + 127 - 7
    else:
        mant, ex = np.frexp(amax / 6.0)
        byte = np.where(mant > 0.5, ex, ex - 1) + 127
    byte = np.clip(np.where(amax > 0, byte, 1), 1, 254)
    scaled = (w * np.exp2(127.0 - byte)[:, None, :]).reshape(k, n).astype(np.float32)
    by_word = np.ascontiguousarray(scaled.reshape(k // 512, 128, 4, n).transpose(0, 1, 3, 2))
    if fmt == "e4m3":
        words = by_word.astype(ml_dtypes.float8_e4m3fn).view(np.uint8)
    else:
        c = by_word.astype(ml_dtypes.float4_e2m1fn).view(np.uint8) & 0xF
        words = (c[..., 0::2] | (c[..., 1::2] << 4)).reshape(k // 512, 128, 2 * n)
    return np.ascontiguousarray(words), np.ascontiguousarray(byte.astype(np.uint8).reshape(k // 512, 16, n))


def unpack_weight(words, scales, fmt):
    g, _, n = scales.shape
    words = np.ascontiguousarray(words).reshape(g, 128, n, -1)
    if fmt == "e4m3":
        vals = words.view(ml_dtypes.float8_e4m3fn).astype(np.float64)
    else:
        nib = np.empty((g, 128, n, 4), np.uint8)
        nib[..., 0::2] = words & 0xF
        nib[..., 1::2] = words >> 4
        vals = E2M1[nib]
    vals = vals * np.repeat(np.exp2(scales.astype(np.float64) - 127.0), 8, axis=1)[..., None]
    return vals.transpose(0, 1, 3, 2).reshape(g * 512, n)


K, J, R, T, C, S, N, Z, U, E = 512, 256, 512, 1024, 512, 128, 256, 1024, 1024, 256


def setup_inputs():
    n = np.random.standard_normal
    idx = np.random.permutation(T)[:J]
    idx2 = np.stack([np.random.permutation(C)[:J] for _ in range(8)])
    idx3 = np.stack([np.random.permutation(C)[:J] for _ in range(8)])
    idx4 = np.stack([np.random.permutation(C)[:S] for _ in range(8)])
    idx5 = np.stack([np.random.permutation(C)[:S] for _ in range(8)])
    idx6 = np.random.permutation(Z)[:N]
    idx7 = np.stack([np.random.permutation(U)[:C] for _ in range(8)])
    fk = mx_kscale(K)
    fr = mx_kscale(R)
    xtp = pack_weight(n((K, T)) * fk[:, None], "e4m3")
    wp = pack_weight(n((K, R)) * 1 / np.sqrt(K) / fk[:, None] * fr, "e4m3")
    w2p = pack_weight(n((K, R)) * 1 / np.sqrt(K) / fk[:, None] * fr, "e2m1")
    vsp = pack_weight(n((R, Z)) * 1 / np.sqrt(R) / fr[:, None], "e2m1")
    return {
        "xt_words": xtp[0],
        "xt_scales": xtp[1],
        "w_words": wp[0],
        "w_scales": wp[1],
        "w2_words": w2p[0],
        "w2_scales": w2p[1],
        "sa": (np.random.uniform(0.5, 1.6, (R, 1))).astype(np.float32),
        "vs_words": vsp[0],
        "vs_scales": vsp[1],
        "offs": striped(idx),
        "offs2": striped8(idx2),
        "offs3": striped8(idx3),
        "offs4": striped8(idx4),
        "offs5": striped8(idx5),
        "offs6": striped(idx6),
        "offs7": striped8(idx7),
    }


def reference(xt_words, xt_scales, w_words, w_scales, w2_words, w2_scales, sa, vs_words, vs_scales, offs, offs2, offs3, offs4, offs5, offs6, offs7):
    idx = unstriped(offs)
    idx2 = unstriped8(offs2)
    idx3 = unstriped8(offs3)
    idx4 = unstriped8(offs4)
    idx5 = unstriped8(offs5)
    idx6 = unstriped(offs6)
    idx7 = unstriped8(offs7)
    xtu = unpack_weight(xt_words, xt_scales, "e4m3")
    wu = unpack_weight(w_words, w_scales, "e4m3")
    w2u = unpack_weight(w2_words, w2_scales, "e2m1")
    vsu = unpack_weight(vs_words, vs_scales, "e2m1")
    xtidxg = xtu[:, idx]
    a = wu.T @ xtidxg
    b = w2u.T @ xtidxg
    pw = np.zeros((R, C))
    pw[np.arange(R)[:, None], idx2[np.arange(R) % 512 // 64]] = a
    pv = np.zeros((R, C))
    pv[np.arange(R)[:, None], idx3[np.arange(R) % 512 // 64]] = b
    h1 = pick8(pw, idx4, 64) * f64(sa)
    pu = np.zeros((R, C))
    pu[np.arange(R)[:, None], idx5[np.arange(R) % 512 // 64]] = h1
    hid = np.abs(pv - pu)
    vsidx6g = vsu[:, idx6]
    hidq = mxq(hid, 0, "e4m3")
    p = vsidx6g.T @ hidq
    m0 = np.zeros((N, U))
    m0[np.arange(N)[:, None], idx7[np.arange(N) % 128 // 16]] = p
    m1 = m0.reshape(N, E, U // E).mean(axis=2)
    m2 = np.repeat(m1, U // E, axis=1)
    y = m0 - m2
    return y

@@ -1,0 +1,229 @@
+from contextlib import ExitStack
+
+import concourse.mybir as mybir
+
+K, J, R, T, C, S, N, Z, U, E = 512, 256, 512, 1024, 512, 128, 256, 1024, 1024, 256
+FLOPS = 2 * K * R * J * 2 + 2 * R * N * C
+
+F32 = mybir.dt.float32
+BF16 = mybir.dt.bfloat16
+I32 = mybir.dt.int32
+U32 = mybir.dt.uint32
+U16 = mybir.dt.uint16
+U8 = mybir.dt.uint8
+FP8X4 = mybir.dt.float8_e4m3fn_x4
+FP4X4 = mybir.dt.float4_e2m1fn_x4
+COPY = mybir.ActivationFunctionType.Copy
+ALU = mybir.AluOpType
+
+P = 128
+PACK = 4
+QUADS = 4
+BUCKET = U // E
+CHUNKS = ((0, 128), (128, 256), (256, 512))
+PAGE_PIECES = ((0, 0, 128), (1, 0, 128), (0, 128, 256), (1, 128, 192), (0, 256, 512), (1, 192, 512))
+STORE = 256
+
+
+def tile_picked_tokens_plain_twin_reposted_store_endcontrast_kernel(
+    tc, xt_words, xt_scales, w_words, w_scales, w2_words, w2_scales, sa, vs_words, vs_scales,
+    offs, offs2, offs3, offs4, offs5, offs6, offs7, out,
+):
+    nc = tc.nc
+    with ExitStack() as ctx:
+        keep = ctx.enter_context(tc.tile_pool(name="keep", bufs=1))
+        psum = ctx.enter_context(tc.psum_pool(name="psum", bufs=4))
+
+        def held_tile(name, shape, dtype, tag=None):
+            return keep.tile(shape, dtype, name=name, tag=tag or name, align_bytes=64)
+
+        def load_list(name, source):
+            held = keep.tile(list(source.shape), U16, name=name)
+            nc.sync.dma_start(held[:], source)
+            return held
+
+        def entries(held, lo, hi):
+            return held[:, lo // 16 : hi // 16]
+
+        def stage_scales(name, queue, source):
+            width = source.shape[2]
+            staged = held_tile(name, [4, QUADS, width // 4], I32)
+            queue.dma_start(staged[:], source[0].rearrange("(q i) w -> i q w", i=4).bitcast(I32))
+            return staged
+
+        def spread_scales(plane, staged):
+            for q in range(QUADS):
+                nc.vector.tensor_copy(plane[32 * q : 32 * q + 4, :].bitcast(I32), staged[:, q, :])
+
+        def load_scales(plane, source):
+            for q in range(QUADS):
+                nc.sync.dma_start(plane[32 * q : 32 * q + 4, :].bitcast(I32), source[0, 4 * q : 4 * q + 4, :].bitcast(I32))
+
+        def zeroed(name, width, dtype, after=None, engine=None):
+            held = held_tile(name, [P, width], dtype, after)
+            (engine or (nc.gpsimd if after else nc.vector)).memset(held[:].bitcast(I32), 0)
+            return held
+
+        xt_plane = zeroed("xt_plane", T, U8)
+        w2_plane = zeroed("w2_plane", R, U8)
+        w_plane = zeroed("w_plane", R, U8)
+        vs_plane = zeroed("vs_plane", Z, U8)
+
+        xt_staged = stage_scales("xt_staged", nc.sync, xt_scales)
+        w2_staged = stage_scales("w2_staged", nc.scalar, w2_scales)
+        idx = load_list("idx", offs)
+        w2_raw = held_tile("w2_raw", [P, R], U16)
+        nc.scalar.dma_start(w2_raw[:].bitcast(I32), w2_words[0].bitcast(I32))
+        idx3 = load_list("idx3", offs3)
+        xt_all = held_tile("xt_all", [P, T], U32)
+        nc.scalar.dma_start(xt_all[:].bitcast(I32), xt_words[0].rearrange("p n t -> p (n t)").bitcast(I32))
+        w_raw = held_tile("w_raw", [P, R], I32)
+        nc.sync.dma_start(w_raw[:], w_words[0].rearrange("p n t -> p (n t)").bitcast(I32))
+        load_scales(w_plane, w_scales)
+        idx2 = load_list("idx2", offs2)
+        idx4 = load_list("idx4", offs4)
+        gains = held_tile("gains", [P, PACK], F32)
+        nc.sync.dma_start(gains[:], sa.rearrange("(p t) o -> p (t o)", t=PACK))
+        idx5 = load_list("idx5", offs5)
+        vs_all = held_tile("vs_all", [P, Z], U16)
+        nc.sync.dma_start(vs_all[:].bitcast(I32), vs_words[0].bitcast(I32))
+        load_scales(vs_plane, vs_scales)
+        idx6 = load_list("idx6", offs6)
+        idx7 = load_list("idx7", offs7)
+
+        spread_scales(xt_plane, xt_staged)
+        spread_scales(w2_plane, w2_staged)
+
+        x_codes = held_tile("x_codes", [P, J], U32)
+        x_scale = held_tile("x_scale", [P, J], U8)
+        w2_codes = held_tile("w2_codes", [P, PACK, P], U16)
+        w2_scale = held_tile("w2_scale", [P, PACK, P], U8)
+        w_codes = held_tile("w_codes", [P, PACK, P], I32)
+        w_scale = held_tile("w_scale", [P, PACK, P], U8)
+
+        def deal(dealt, raw, lo, hi):
+            nc.vector.tensor_copy(dealt[:, lo:hi, :], raw[:].rearrange("p (m t) -> p t m", t=PACK)[:, lo:hi, :])
+
+        def gather_x(dst, window, lo, hi):
+            nc.vector.tensor_copy(dst[:, lo:hi], window[:].indirect(entries(idx, lo, hi)))
+
+        def product(name, codes, scale, fmt, t, lo, hi):
+            acc = psum.tile([P, hi - lo], F32, name="first_acc")
+            nc.tensor.matmul_mx(
+                out=acc[:], lhsT=codes[:, t, :].bitcast(fmt), lhsT_scale=scale[:, t, :],
+                rhs=x_codes[:, lo:hi].bitcast(FP8X4), rhs_scale=x_scale[:, lo:hi], start=True, stop=True,
+            )
+            held = held_tile(name, [P, hi - lo], F32)
+            nc.vector.tensor_copy(held[:], acc[:])
+            return held
+
+        def scatter(board, held, lo, hi, values):
+            nc.scalar.activation(board[:].indirect(entries(held, lo, hi)), values, COPY)
+
+        pv = [None] * PACK
+        pw = [None] * PACK
+        pu = [None] * PACK
+        h1 = [None] * PACK
+        diff = [held_tile("diff%d" % i, [P, PACK, hi - lo], F32) for i, (lo, hi) in enumerate(CHUNKS)]
+        hid = [held_tile("hid%d" % i, [P, hi - lo, PACK], BF16) for i, (lo, hi) in enumerate(CHUNKS)]
+
+        def put_b(t, lo, hi):
+            if pv[t] is None:
+                pv[t] = zeroed("pv%d" % t, C, F32, (None, None, "a2", "a3")[t])
+            scatter(pv[t], idx3, lo, hi, product("b%d_%d" % (t, lo), w2_codes, w2_scale, FP4X4, t, lo, hi)[:])
+
+        def put_a(t):
+            pw[t] = zeroed("pw%d" % t, C, F32, (None, None, "b0_128", "b1_128")[t], nc.gpsimd)
+            scatter(pw[t], idx2, 0, J, product("a%d" % t, w_codes, w_scale, FP8X4, t, 0, J)[:])
+
+        def pick(t):
+            h1[t] = held_tile("h1_%d" % t, [P, S], F32)
+            nc.scalar.activation(h1[t][:], pw[t][:].indirect(idx4[:]), COPY, scale=gains[:, t : t + 1])
+
+        def put_u(t):
+            pu[t] = zeroed("pu%d" % t, C, F32, ("a0", "a1", "pw0", "pw1")[t])
+            scatter(pu[t], idx5, 0, S, h1[t][:])
+
+        def subtract(t, i):
+            lo, hi = CHUNKS[i]
+            nc.vector.tensor_tensor(diff[i][:, t, :], pv[t][:, lo:hi], pu[t][:, lo:hi], ALU.subtract)
+
+        def magnitude(t, i):
+            pair = diff[i][:, t : t + 2, :].rearrange("p t c -> p c t")
+            nc.vector.scalar_tensor_tensor(hid[i][:, :, t : t + 2], pair, -1.0, pair, ALU.mult, ALU.max)
+
+        half = J // 2
+        gather_x(x_scale, xt_plane, 0, half)
+        deal(w2_scale, w2_plane, 0, 1)
+        deal(w2_codes, w2_raw, 0, 1)
+        gather_x(x_codes, xt_all, 0, half)
+        put_b(0, 0, half)
+        deal(w2_scale, w2_plane, 1, 2)
+        deal(w2_codes, w2_raw, 1, 2)
+        put_b(1, 0, half)
+        gather_x(x_scale, xt_plane, half, J)
+        gather_x(x_codes, xt_all, half, J)
+        put_b(0, half, J)
+        put_b(1, half, J)
+        deal(w_codes, w_raw, 0, PACK)
+        deal(w_scale, w_plane, 0, PACK)
+        put_a(0)
+        put_a(1)
+        deal(w2_scale, w2_plane, 2, PACK)
+        deal(w2_codes, w2_raw, 2, PACK)
+        pick(0)
+        put_a(2)
+        put_u(0)
+        pick(1)
+        put_a(3)
+        put_u(1)
+        pick(2)
+        put_b(2, 0, J)
+        put_u(2)
+        pick(3)
+        put_b(3, 0, J)
+        put_u(3)
+
+        v_codes = held_tile("v_codes", [P, N], U16)
+        v_scale = held_tile("v_scale", [P, N], U8)
+        nc.vector.tensor_copy(v_codes[:], vs_all[:].indirect(idx6[:]))
+        nc.vector.tensor_copy(v_scale[:], vs_plane[:].indirect(idx6[:]))
+        page = [zeroed("page%d" % g, U, F32, "h1_%d" % g) for g in range(N // P)]
+
+        for t in range(PACK - 1):
+            for i in range(len(CHUNKS)):
+                subtract(t, i)
+            if t == 1:
+                for i in range(len(CHUNKS)):
+                    magnitude(0, i)
+
+        last = [held_tile("last%d" % g, [P, C], F32) for g in range(N // P)]
+        for i, (lo, hi) in enumerate(CHUNKS):
+            subtract(PACK - 1, i)
+            magnitude(2, i)
+            h_codes = held_tile("h_codes%d" % i, [P, hi - lo], U32)
+            h_scale = held_tile("h_scale%d" % i, [P, hi - lo], U8)
+            nc.vector.quantize_mx(out=h_codes[:].bitcast(FP8X4), scales=h_scale[:], in_=hid[i][:].rearrange("p c t -> p (c t)"))
+            for g in range(N // P):
+                acc = psum.tile([P, hi - lo], F32, name="last_acc")
+                nc.tensor.matmul_mx(
+                    out=acc[:], lhsT=v_codes[:, g * P : (g + 1) * P].bitcast(FP4X4), lhsT_scale=v_scale[:, g * P : (g + 1) * P],
+                    rhs=h_codes[:].bitcast(FP8X4), rhs_scale=h_scale[:], start=True, stop=True,
+                )
+                nc.vector.tensor_copy(last[g][:, lo:hi], acc[:])
+
+        for g, lo, hi in PAGE_PIECES:
+            scatter(page[g], idx7, lo, hi, last[g][:, lo:hi])
+
+        for g in range(N // P):
+            for u0 in range(0, U, STORE):
+                buckets = page[g][:, u0 : u0 + STORE].rearrange("p (e j) -> p e j", j=BUCKET)
+                pairs = held_tile("pairs%d_%d" % (g, u0), [P, STORE // BUCKET, 2], F32)
+                nc.vector.tensor_tensor(pairs[:], buckets[:, :, 0:2], buckets[:, :, 2:4], ALU.add)
+                sums = held_tile("sums%d_%d" % (g, u0), [P, STORE // BUCKET], F32)
+                nc.vector.tensor_tensor(sums[:], pairs[:, :, 0], pairs[:, :, 1], ALU.add)
+                result = held_tile("result%d_%d" % (g, u0), [P, STORE // BUCKET, BUCKET], F32)
+                nc.vector.scalar_tensor_tensor(
+                    result[:], sums[:].unsqueeze(2).to_broadcast([P, STORE // BUCKET, BUCKET]), -1.0 / BUCKET, buckets, ALU.mult, ALU.add
+                )
+                nc.sync.dma_start(out[g * P : (g + 1) * P, u0 : u0 + STORE], result[:].rearrange("p e j -> p (e j)"))

@@ -21,8 +21,8 @@ PACK = 4
 QUADS = 4
 BUCKET = U // E
 CHUNKS = ((0, 128), (128, 256), (256, 512))
-PAGE_PIECES = ((0, 0, 128), (1, 0, 128), (0, 128, 256), (1, 128, 192), (0, 256, 512), (1, 192, 512))
-STORE = 256
+PAGE_PIECES = ((0, 0, 128), (1, 0, 128), (0, 128, 512), (1, 128, 512))
+STORES = ((0, 96), (96, 176), (176, 224), (224, 256))
 
 
 def tile_picked_tokens_plain_twin_reposted_store_endcontrast_kernel(
@@ -64,19 +64,19 @@ def tile_picked_tokens_plain_twin_reposted_store_endcontrast_kernel(
             (engine or (nc.gpsimd if after else nc.vector)).memset(held[:].bitcast(I32), 0)
             return held
 
-        xt_plane = zeroed("xt_plane", T, U8)
         w2_plane = zeroed("w2_plane", R, U8)
+        xt_plane = zeroed("xt_plane", T, U8)
         w_plane = zeroed("w_plane", R, U8)
         vs_plane = zeroed("vs_plane", Z, U8)
 
         xt_staged = stage_scales("xt_staged", nc.sync, xt_scales)
-        w2_staged = stage_scales("w2_staged", nc.scalar, w2_scales)
-        idx = load_list("idx", offs)
         w2_raw = held_tile("w2_raw", [P, R], U16)
         nc.scalar.dma_start(w2_raw[:].bitcast(I32), w2_words[0].bitcast(I32))
-        idx3 = load_list("idx3", offs3)
+        idx = load_list("idx", offs)
         xt_all = held_tile("xt_all", [P, T], U32)
         nc.scalar.dma_start(xt_all[:].bitcast(I32), xt_words[0].rearrange("p n t -> p (n t)").bitcast(I32))
+        load_scales(w2_plane, w2_scales)
+        idx3 = load_list("idx3", offs3)
         w_raw = held_tile("w_raw", [P, R], I32)
         nc.sync.dma_start(w_raw[:], w_words[0].rearrange("p n t -> p (n t)").bitcast(I32))
         load_scales(w_plane, w_scales)
@@ -92,17 +92,14 @@ def tile_picked_tokens_plain_twin_reposted_store_endcontrast_kernel(
         idx7 = load_list("idx7", offs7)
 
         spread_scales(xt_plane, xt_staged)
-        spread_scales(w2_plane, w2_staged)
 
         x_codes = held_tile("x_codes", [P, J], U32)
         x_scale = held_tile("x_scale", [P, J], U8)
-        w2_codes = held_tile("w2_codes", [P, PACK, P], U16)
-        w2_scale = held_tile("w2_scale", [P, PACK, P], U8)
-        w_codes = held_tile("w_codes", [P, PACK, P], I32)
-        w_scale = held_tile("w_scale", [P, PACK, P], U8)
 
-        def deal(dealt, raw, lo, hi):
-            nc.vector.tensor_copy(dealt[:, lo:hi, :], raw[:].rearrange("p (m t) -> p t m", t=PACK)[:, lo:hi, :])
+        def deal(name, move, raw, lo, hi, after=None):
+            dealt = held_tile(name, [P, hi - lo, P], raw.dtype, after)
+            move(dealt[:], raw[:].rearrange("p (m t) -> p t m", t=PACK)[:, lo:hi, :])
+            return [dealt[:, t, :] for t in range(hi - lo)]
 
         def gather_x(dst, window, lo, hi):
             nc.vector.tensor_copy(dst[:, lo:hi], window[:].indirect(entries(idx, lo, hi)))
@@ -110,7 +107,7 @@ def tile_picked_tokens_plain_twin_reposted_store_endcontrast_kernel(
         def product(name, codes, scale, fmt, t, lo, hi):
             acc = psum.tile([P, hi - lo], F32, name="first_acc")
             nc.tensor.matmul_mx(
-                out=acc[:], lhsT=codes[:, t, :].bitcast(fmt), lhsT_scale=scale[:, t, :],
+                out=acc[:], lhsT=codes[t].bitcast(fmt), lhsT_scale=scale[t],
                 rhs=x_codes[:, lo:hi].bitcast(FP8X4), rhs_scale=x_scale[:, lo:hi], start=True, stop=True,
             )
             held = held_tile(name, [P, hi - lo], F32)
@@ -124,8 +121,6 @@ def tile_picked_tokens_plain_twin_reposted_store_endcontrast_kernel(
         pw = [None] * PACK
         pu = [None] * PACK
         h1 = [None] * PACK
-        diff = [held_tile("diff%d" % i, [P, PACK, hi - lo], F32) for i, (lo, hi) in enumerate(CHUNKS)]
-        hid = [held_tile("hid%d" % i, [P, hi - lo, PACK], BF16) for i, (lo, hi) in enumerate(CHUNKS)]
 
         def put_b(t, lo, hi):
             if pv[t] is None:
@@ -144,33 +139,22 @@ def tile_picked_tokens_plain_twin_reposted_store_endcontrast_kernel(
             pu[t] = zeroed("pu%d" % t, C, F32, ("a0", "a1", "pw0", "pw1")[t])
             scatter(pu[t], idx5, 0, S, h1[t][:])
 
-        def subtract(t, i):
-            lo, hi = CHUNKS[i]
-            nc.vector.tensor_tensor(diff[i][:, t, :], pv[t][:, lo:hi], pu[t][:, lo:hi], ALU.subtract)
-
-        def magnitude(t, i):
-            pair = diff[i][:, t : t + 2, :].rearrange("p t c -> p c t")
-            nc.vector.scalar_tensor_tensor(hid[i][:, :, t : t + 2], pair, -1.0, pair, ALU.mult, ALU.max)
-
         half = J // 2
-        gather_x(x_scale, xt_plane, 0, half)
-        deal(w2_scale, w2_plane, 0, 1)
-        deal(w2_codes, w2_raw, 0, 1)
+        w2_scale = deal("w2_scale01", nc.gpsimd.tensor_copy, w2_plane, 0, 2)
+        w2_codes = deal("w2_codes01", nc.scalar.copy, w2_raw, 0, 2)
+        gather_x(x_scale, xt_plane, 0, J)
         gather_x(x_codes, xt_all, 0, half)
         put_b(0, 0, half)
-        deal(w2_scale, w2_plane, 1, 2)
-        deal(w2_codes, w2_raw, 1, 2)
         put_b(1, 0, half)
-        gather_x(x_scale, xt_plane, half, J)
         gather_x(x_codes, xt_all, half, J)
         put_b(0, half, J)
         put_b(1, half, J)
-        deal(w_codes, w_raw, 0, PACK)
-        deal(w_scale, w_plane, 0, PACK)
+        w_codes = deal("w_codes", nc.vector.tensor_copy, w_raw, 0, PACK)
+        w_scale = deal("w_scale", nc.vector.tensor_copy, w_plane, 0, PACK)
         put_a(0)
         put_a(1)
-        deal(w2_scale, w2_plane, 2, PACK)
-        deal(w2_codes, w2_raw, 2, PACK)
+        w2_scale.extend(deal("w2_scale23", nc.vector.tensor_copy, w2_plane, 2, PACK, "b0_0"))
+        w2_codes.extend(deal("w2_codes23", nc.vector.tensor_copy, w2_raw, 2, PACK, "b1_0"))
         pick(0)
         put_a(2)
         put_u(0)
@@ -190,20 +174,31 @@ def tile_picked_tokens_plain_twin_reposted_store_endcontrast_kernel(
         nc.vector.tensor_copy(v_scale[:], vs_plane[:].indirect(idx6[:]))
         page = [zeroed("page%d" % g, U, F32, "h1_%d" % g) for g in range(N // P)]
 
-        for t in range(PACK - 1):
-            for i in range(len(CHUNKS)):
-                subtract(t, i)
-            if t == 1:
-                for i in range(len(CHUNKS)):
-                    magnitude(0, i)
+        diff = held_tile("diff", [P, 2, C], F32, "vs_all")
+        hid = held_tile("hid", [P, C, PACK], BF16, "vs_plane")
+
+        def subtract(t, lo, hi):
+            nc.vector.tensor_tensor(diff[:, t % 2, lo:hi], pv[t][:, lo:hi], pu[t][:, lo:hi], ALU.subtract)
+
+        def magnitude(t, lo, hi):
+            pair = diff[:, :, lo:hi].rearrange("p t c -> p c t")
+            nc.vector.scalar_tensor_tensor(hid[:, lo:hi, t : t + 2], pair, -1.0, pair, ALU.mult, ALU.max)
+
+        subtract(0, 0, C)
+        subtract(1, 0, C)
+        magnitude(0, 0, C)
+        subtract(2, 0, C)
 
         last = [held_tile("last%d" % g, [P, C], F32) for g in range(N // P)]
         for i, (lo, hi) in enumerate(CHUNKS):
-            subtract(PACK - 1, i)
-            magnitude(2, i)
+            subtract(PACK - 1, lo, hi)
+            if i == 0:
+                magnitude(2, lo, hi)
+            else:
+                nc.scalar.activation(hid[:, lo:hi, 2:4], diff[:, :, lo:hi].rearrange("p t c -> p c t"), mybir.ActivationFunctionType.Abs)
             h_codes = held_tile("h_codes%d" % i, [P, hi - lo], U32)
             h_scale = held_tile("h_scale%d" % i, [P, hi - lo], U8)
-            nc.vector.quantize_mx(out=h_codes[:].bitcast(FP8X4), scales=h_scale[:], in_=hid[i][:].rearrange("p c t -> p (c t)"))
+            nc.vector.quantize_mx(out=h_codes[:].bitcast(FP8X4), scales=h_scale[:], in_=hid[:, lo:hi, :].rearrange("p c t -> p (c t)"))
             for g in range(N // P):
                 acc = psum.tile([P, hi - lo], F32, name="last_acc")
                 nc.tensor.matmul_mx(
@@ -216,14 +211,19 @@ def tile_picked_tokens_plain_twin_reposted_store_endcontrast_kernel(
             scatter(page[g], idx7, lo, hi, last[g][:, lo:hi])
 
         for g in range(N // P):
-            for u0 in range(0, U, STORE):
-                buckets = page[g][:, u0 : u0 + STORE].rearrange("p (e j) -> p e j", j=BUCKET)
-                pairs = held_tile("pairs%d_%d" % (g, u0), [P, STORE // BUCKET, 2], F32)
-                nc.vector.tensor_tensor(pairs[:], buckets[:, :, 0:2], buckets[:, :, 2:4], ALU.add)
-                sums = held_tile("sums%d_%d" % (g, u0), [P, STORE // BUCKET], F32)
-                nc.vector.tensor_tensor(sums[:], pairs[:, :, 0], pairs[:, :, 1], ALU.add)
-                result = held_tile("result%d_%d" % (g, u0), [P, STORE // BUCKET, BUCKET], F32)
+            buckets = page[g][:].rearrange("p (e j) -> p e j", j=BUCKET)
+            pairs = held_tile("pairs%d" % g, [P, E, 2], F32)
+            sums = held_tile("sums%d" % g, [P, E], F32)
+            result = held_tile("result%d" % g, [P, E, BUCKET], F32)
+            for lo, hi in ((0, E // 2), (E // 2, E)):
+                nc.vector.tensor_tensor(pairs[:, lo:hi, :], buckets[:, lo:hi, 0:2], buckets[:, lo:hi, 2:4], ALU.add)
+            for lo, hi in ((0, E // 2), (E // 2, E)):
+                nc.vector.tensor_tensor(sums[:, lo:hi], pairs[:, lo:hi, 0], pairs[:, lo:hi, 1], ALU.add)
+            for lo, hi in STORES:
                 nc.vector.scalar_tensor_tensor(
-                    result[:], sums[:].unsqueeze(2).to_broadcast([P, STORE // BUCKET, BUCKET]), -1.0 / BUCKET, buckets, ALU.mult, ALU.add
+                    result[:, lo:hi, :], sums[:, lo:hi].unsqueeze(2).to_broadcast([P, hi - lo, BUCKET]), -1.0 / BUCKET,
+                    buckets[:, lo:hi, :], ALU.mult, ALU.add,
                 )
-                nc.sync.dma_start(out[g * P : (g + 1) * P, u0 : u0 + STORE], result[:].rearrange("p e j -> p (e j)"))
+                nc.sync.dma_start(
+                    out[g * P : (g + 1) * P, lo * BUCKET : hi * BUCKET], result[:, lo:hi, :].rearrange("p e j -> p (e j)")
+                )

@@ -64,21 +64,21 @@ def tile_picked_tokens_plain_twin_reposted_store_endcontrast_kernel(
             (engine or (nc.gpsimd if after else nc.vector)).memset(held[:].bitcast(I32), 0)
             return held
 
-        w2_plane = zeroed("w2_plane", R, U8)
         xt_plane = zeroed("xt_plane", T, U8)
+        w2_plane = zeroed("w2_plane", R, U8)
         w_plane = zeroed("w_plane", R, U8)
         vs_plane = zeroed("vs_plane", Z, U8)
 
         xt_staged = stage_scales("xt_staged", nc.sync, xt_scales)
-        w2_raw = held_tile("w2_raw", [P, R], U16)
-        nc.scalar.dma_start(w2_raw[:].bitcast(I32), w2_words[0].bitcast(I32))
+        w2_staged = stage_scales("w2_staged", nc.scalar, w2_scales)
         idx = load_list("idx", offs)
         xt_all = held_tile("xt_all", [P, T], U32)
         nc.scalar.dma_start(xt_all[:].bitcast(I32), xt_words[0].rearrange("p n t -> p (n t)").bitcast(I32))
-        load_scales(w2_plane, w2_scales)
         idx3 = load_list("idx3", offs3)
+        w2_raw = held_tile("w2_raw", [P, R], U16)
+        nc.scalar.dma_start(w2_raw[:].bitcast(I32), w2_words[0].bitcast(I32))
         w_raw = held_tile("w_raw", [P, R], I32)
-        nc.sync.dma_start(w_raw[:], w_words[0].rearrange("p n t -> p (n t)").bitcast(I32))
+        nc.scalar.dma_start(w_raw[:], w_words[0].rearrange("p n t -> p (n t)").bitcast(I32))
         load_scales(w_plane, w_scales)
         idx2 = load_list("idx2", offs2)
         idx4 = load_list("idx4", offs4)
@@ -91,6 +91,7 @@ def tile_picked_tokens_plain_twin_reposted_store_endcontrast_kernel(
         idx6 = load_list("idx6", offs6)
         idx7 = load_list("idx7", offs7)
 
+        spread_scales(w2_plane, w2_staged)
         spread_scales(xt_plane, xt_staged)
 
         x_codes = held_tile("x_codes", [P, J], U32)
@@ -124,7 +125,7 @@ def tile_picked_tokens_plain_twin_reposted_store_endcontrast_kernel(
 
         def put_b(t, lo, hi):
             if pv[t] is None:
-                pv[t] = zeroed("pv%d" % t, C, F32, (None, None, "a2", "a3")[t])
+                pv[t] = zeroed("pv%d" % t, C, F32, (None, None, "a2", "a3")[t], nc.gpsimd if t else nc.vector)
             scatter(pv[t], idx3, lo, hi, product("b%d_%d" % (t, lo), w2_codes, w2_scale, FP4X4, t, lo, hi)[:])
 
         def put_a(t):
@@ -140,12 +141,15 @@ def tile_picked_tokens_plain_twin_reposted_store_endcontrast_kernel(
             scatter(pu[t], idx5, 0, S, h1[t][:])
 
         half = J // 2
-        w2_scale = deal("w2_scale01", nc.gpsimd.tensor_copy, w2_plane, 0, 2)
-        w2_codes = deal("w2_codes01", nc.scalar.copy, w2_raw, 0, 2)
-        gather_x(x_scale, xt_plane, 0, J)
+        w2_scale = deal("w2_scale0", nc.vector.tensor_copy, w2_plane, 0, 1)
+        w2_codes = deal("w2_codes0", nc.scalar.copy, w2_raw, 0, 1)
+        w2_codes.extend(deal("w2_codes1", nc.scalar.copy, w2_raw, 1, 2))
+        gather_x(x_scale, xt_plane, 0, half)
         gather_x(x_codes, xt_all, 0, half)
         put_b(0, 0, half)
+        w2_scale.extend(deal("w2_scale1", nc.vector.tensor_copy, w2_plane, 1, 2))
         put_b(1, 0, half)
+        gather_x(x_scale, xt_plane, half, J)
         gather_x(x_codes, xt_all, half, J)
         put_b(0, half, J)
         put_b(1, half, J)
@@ -212,7 +216,7 @@ def tile_picked_tokens_plain_twin_reposted_store_endcontrast_kernel(
 
         for g in range(N // P):
             buckets = page[g][:].rearrange("p (e j) -> p e j", j=BUCKET)
-            pairs = held_tile("pairs%d" % g, [P, E, 2], F32)
+            pairs = held_tile("pairs%d" % g, [P, E, 2], F32, "sums0" if g else None)
             sums = held_tile("sums%d" % g, [P, E], F32)
             result = held_tile("result%d" % g, [P, E, BUCKET], F32)
             for lo, hi in ((0, E // 2), (E // 2, E)):

from contextlib import ExitStack

import concourse.mybir as mybir

K, J, R, T, C, S, N, Z, U, E = 512, 256, 512, 1024, 512, 128, 256, 1024, 1024, 256
FLOPS = 2 * K * R * J * 2 + 2 * R * N * C

F32 = mybir.dt.float32
BF16 = mybir.dt.bfloat16
I32 = mybir.dt.int32
U32 = mybir.dt.uint32
U16 = mybir.dt.uint16
U8 = mybir.dt.uint8
FP8X4 = mybir.dt.float8_e4m3fn_x4
FP4X4 = mybir.dt.float4_e2m1fn_x4
COPY = mybir.ActivationFunctionType.Copy
ALU = mybir.AluOpType

P = 128
PACK = 4
QUADS = 4
BUCKET = U // E
CHUNKS = ((0, 128), (128, 256), (256, 512))
PAGE_PIECES = ((0, 0, 128), (1, 0, 128), (0, 128, 512), (1, 128, 512))
STORES = ((0, 96), (96, 176), (176, 224), (224, 256))


def tile_picked_tokens_plain_twin_reposted_store_endcontrast_kernel(
    tc, xt_words, xt_scales, w_words, w_scales, w2_words, w2_scales, sa, vs_words, vs_scales,
    offs, offs2, offs3, offs4, offs5, offs6, offs7, out,
):
    nc = tc.nc
    with ExitStack() as ctx:
        keep = ctx.enter_context(tc.tile_pool(name="keep", bufs=1))
        psum = ctx.enter_context(tc.psum_pool(name="psum", bufs=4))

        def held_tile(name, shape, dtype, tag=None):
            return keep.tile(shape, dtype, name=name, tag=tag or name, align_bytes=64)

        def load_list(name, source):
            held = keep.tile(list(source.shape), U16, name=name)
            nc.sync.dma_start(held[:], source)
            return held

        def entries(held, lo, hi):
            return held[:, lo // 16 : hi // 16]

        def stage_scales(name, queue, source):
            width = source.shape[2]
            staged = held_tile(name, [4, QUADS, width // 4], I32)
            queue.dma_start(staged[:], source[0].rearrange("(q i) w -> i q w", i=4).bitcast(I32))
            return staged

        def spread_scales(plane, staged):
            for q in range(QUADS):
                nc.vector.tensor_copy(plane[32 * q : 32 * q + 4, :].bitcast(I32), staged[:, q, :])

        def load_scales(plane, source):
            for q in range(QUADS):
                nc.sync.dma_start(plane[32 * q : 32 * q + 4, :].bitcast(I32), source[0, 4 * q : 4 * q + 4, :].bitcast(I32))

        def zeroed(name, width, dtype, after=None, engine=None):
            held = held_tile(name, [P, width], dtype, after)
            (engine or (nc.gpsimd if after else nc.vector)).memset(held[:].bitcast(I32), 0)
            return held

        xt_plane = zeroed("xt_plane", T, U8)
        w2_plane = zeroed("w2_plane", R, U8)
        w_plane = zeroed("w_plane", R, U8)
        vs_plane = zeroed("vs_plane", Z, U8)

        xt_staged = stage_scales("xt_staged", nc.sync, xt_scales)
        w2_staged = stage_scales("w2_staged", nc.scalar, w2_scales)
        idx = load_list("idx", offs)
        xt_all = held_tile("xt_all", [P, T], U32)
        nc.scalar.dma_start(xt_all[:].bitcast(I32), xt_words[0].rearrange("p n t -> p (n t)").bitcast(I32))
        idx3 = load_list("idx3", offs3)
        w2_raw = held_tile("w2_raw", [P, R], U16)
        nc.scalar.dma_start(w2_raw[:].bitcast(I32), w2_words[0].bitcast(I32))
        w_raw = held_tile("w_raw", [P, R], I32)
        nc.scalar.dma_start(w_raw[:], w_words[0].rearrange("p n t -> p (n t)").bitcast(I32))
        load_scales(w_plane, w_scales)
        idx2 = load_list("idx2", offs2)
        idx4 = load_list("idx4", offs4)
        gains = held_tile("gains", [P, PACK], F32)
        nc.sync.dma_start(gains[:], sa.rearrange("(p t) o -> p (t o)", t=PACK))
        idx5 = load_list("idx5", offs5)
        vs_all = held_tile("vs_all", [P, Z], U16)
        nc.sync.dma_start(vs_all[:].bitcast(I32), vs_words[0].bitcast(I32))
        load_scales(vs_plane, vs_scales)
        idx6 = load_list("idx6", offs6)
        idx7 = load_list("idx7", offs7)

        spread_scales(w2_plane, w2_staged)
        spread_scales(xt_plane, xt_staged)

        x_codes = held_tile("x_codes", [P, J], U32)
        x_scale = held_tile("x_scale", [P, J], U8)

        def deal(name, move, raw, lo, hi, after=None):
            dealt = held_tile(name, [P, hi - lo, P], raw.dtype, after)
            move(dealt[:], raw[:].rearrange("p (m t) -> p t m", t=PACK)[:, lo:hi, :])
            return [dealt[:, t, :] for t in range(hi - lo)]

        def gather_x(dst, window, lo, hi):
            nc.vector.tensor_copy(dst[:, lo:hi], window[:].indirect(entries(idx, lo, hi)))

        def product(name, codes, scale, fmt, t, lo, hi):
            acc = psum.tile([P, hi - lo], F32, name="first_acc")
            nc.tensor.matmul_mx(
                out=acc[:], lhsT=codes[t].bitcast(fmt), lhsT_scale=scale[t],
                rhs=x_codes[:, lo:hi].bitcast(FP8X4), rhs_scale=x_scale[:, lo:hi], start=True, stop=True,
            )
            held = held_tile(name, [P, hi - lo], F32)
            nc.vector.tensor_copy(held[:], acc[:])
            return held

        def scatter(board, held, lo, hi, values):
            nc.scalar.activation(board[:].indirect(entries(held, lo, hi)), values, COPY)

        pv = [None] * PACK
        pw = [None] * PACK
        pu = [None] * PACK
        h1 = [None] * PACK

        def put_b(t, lo, hi):
            if pv[t] is None:
                pv[t] = zeroed("pv%d" % t, C, F32, (None, None, "a2", "a3")[t], nc.gpsimd if t else nc.vector)
            scatter(pv[t], idx3, lo, hi, product("b%d_%d" % (t, lo), w2_codes, w2_scale, FP4X4, t, lo, hi)[:])

        def put_a(t):
            pw[t] = zeroed("pw%d" % t, C, F32, (None, None, "b0_128", "b1_128")[t], nc.gpsimd)
            scatter(pw[t], idx2, 0, J, product("a%d" % t, w_codes, w_scale, FP8X4, t, 0, J)[:])

        def pick(t):
            h1[t] = held_tile("h1_%d" % t, [P, S], F32)
            nc.scalar.activation(h1[t][:], pw[t][:].indirect(idx4[:]), COPY, scale=gains[:, t : t + 1])

        def put_u(t):
            pu[t] = zeroed("pu%d" % t, C, F32, ("a0", "a1", "pw0", "pw1")[t])
            scatter(pu[t], idx5, 0, S, h1[t][:])

        half = J // 2
        w2_scale = deal("w2_scale0", nc.vector.tensor_copy, w2_plane, 0, 1)
        w2_codes = deal("w2_codes0", nc.scalar.copy, w2_raw, 0, 1)
        w2_codes.extend(deal("w2_codes1", nc.scalar.copy, w2_raw, 1, 2))
        gather_x(x_scale, xt_plane, 0, half)
        gather_x(x_codes, xt_all, 0, half)
        put_b(0, 0, half)
        w2_scale.extend(deal("w2_scale1", nc.vector.tensor_copy, w2_plane, 1, 2))
        put_b(1, 0, half)
        gather_x(x_scale, xt_plane, half, J)
        gather_x(x_codes, xt_all, half, J)
        put_b(0, half, J)
        put_b(1, half, J)
        w_codes = deal("w_codes", nc.vector.tensor_copy, w_raw, 0, PACK)
        w_scale = deal("w_scale", nc.vector.tensor_copy, w_plane, 0, PACK)
        put_a(0)
        put_a(1)
        w2_scale.extend(deal("w2_scale23", nc.vector.tensor_copy, w2_plane, 2, PACK, "b0_0"))
        w2_codes.extend(deal("w2_codes23", nc.vector.tensor_copy, w2_raw, 2, PACK, "b1_0"))
        pick(0)
        put_a(2)
        put_u(0)
        pick(1)
        put_a(3)
        put_u(1)
        pick(2)
        put_b(2, 0, J)
        put_u(2)
        pick(3)
        put_b(3, 0, J)
        put_u(3)

        v_codes = held_tile("v_codes", [P, N], U16)
        v_scale = held_tile("v_scale", [P, N], U8)
        nc.vector.tensor_copy(v_codes[:], vs_all[:].indirect(idx6[:]))
        nc.vector.tensor_copy(v_scale[:], vs_plane[:].indirect(idx6[:]))
        page = [zeroed("page%d" % g, U, F32, "h1_%d" % g) for g in range(N // P)]

        diff = held_tile("diff", [P, 2, C], F32, "vs_all")
        hid = held_tile("hid", [P, C, PACK], BF16, "vs_plane")

        def subtract(t, lo, hi):
            nc.vector.tensor_tensor(diff[:, t % 2, lo:hi], pv[t][:, lo:hi], pu[t][:, lo:hi], ALU.subtract)

        def magnitude(t, lo, hi):
            pair = diff[:, :, lo:hi].rearrange("p t c -> p c t")
            nc.vector.scalar_tensor_tensor(hid[:, lo:hi, t : t + 2], pair, -1.0, pair, ALU.mult, ALU.max)

        subtract(0, 0, C)
        subtract(1, 0, C)
        magnitude(0, 0, C)
        subtract(2, 0, C)

        last = [held_tile("last%d" % g, [P, C], F32) for g in range(N // P)]
        for i, (lo, hi) in enumerate(CHUNKS):
            subtract(PACK - 1, lo, hi)
            if i == 0:
                magnitude(2, lo, hi)
            else:
                nc.scalar.activation(hid[:, lo:hi, 2:4], diff[:, :, lo:hi].rearrange("p t c -> p c t"), mybir.ActivationFunctionType.Abs)
            h_codes = held_tile("h_codes%d" % i, [P, hi - lo], U32)
            h_scale = held_tile("h_scale%d" % i, [P, hi - lo], U8)
            nc.vector.quantize_mx(out=h_codes[:].bitcast(FP8X4), scales=h_scale[:], in_=hid[:, lo:hi, :].rearrange("p c t -> p (c t)"))
            for g in range(N // P):
                acc = psum.tile([P, hi - lo], F32, name="last_acc")
                nc.tensor.matmul_mx(
                    out=acc[:], lhsT=v_codes[:, g * P : (g + 1) * P].bitcast(FP4X4), lhsT_scale=v_scale[:, g * P : (g + 1) * P],
                    rhs=h_codes[:].bitcast(FP8X4), rhs_scale=h_scale[:], start=True, stop=True,
                )
                nc.vector.tensor_copy(last[g][:, lo:hi], acc[:])

        for g, lo, hi in PAGE_PIECES:
            scatter(page[g], idx7, lo, hi, last[g][:, lo:hi])

        for g in range(N // P):
            buckets = page[g][:].rearrange("p (e j) -> p e j", j=BUCKET)
            pairs = held_tile("pairs%d" % g, [P, E, 2], F32, "sums0" if g else None)
            sums = held_tile("sums%d" % g, [P, E], F32)
            result = held_tile("result%d" % g, [P, E, BUCKET], F32)
            for lo, hi in ((0, E // 2), (E // 2, E)):
                nc.vector.tensor_tensor(pairs[:, lo:hi, :], buckets[:, lo:hi, 0:2], buckets[:, lo:hi, 2:4], ALU.add)
            for lo, hi in ((0, E // 2), (E // 2, E)):
                nc.vector.tensor_tensor(sums[:, lo:hi], pairs[:, lo:hi, 0], pairs[:, lo:hi, 1], ALU.add)
            for lo, hi in STORES:
                nc.vector.scalar_tensor_tensor(
                    result[:, lo:hi, :], sums[:, lo:hi].unsqueeze(2).to_broadcast([P, hi - lo, BUCKET]), -1.0 / BUCKET,
                    buckets[:, lo:hi, :], ALU.mult, ALU.add,
                )
                nc.sync.dma_start(
                    out[g * P : (g + 1) * P, lo * BUCKET : hi * BUCKET], result[:, lo:hi, :].rearrange("p e j -> p (e j)")
                )
